import numpy as np
import ml_dtypes


def mxq(x, axis, fmt="e4m3"):
    dtype, down = {"e4m3": (ml_dtypes.float8_e4m3fn, 7), "e5m2": (ml_dtypes.float8_e5m2, 14)}[fmt]
    v = np.moveaxis(np.asarray(x, np.float32).astype(ml_dtypes.bfloat16).astype(np.float64), axis, -1)
    blocks = v.reshape(v.shape[:-1] + (-1, 32))
    amax = np.abs(blocks).max(-1, keepdims=True)
    byte = np.maximum(np.where(amax > 0, np.frexp(amax)[1] - 1 + 127, 0) - down, 1)
    scale = np.exp2(byte - 127.0)
    codes = (blocks / scale).astype(np.float32).astype(dtype).astype(np.float64)
    return np.moveaxis((codes * scale).reshape(v.shape), -1, axis)


WIDE = False


def mx_kscale(k):
    if not WIDE:
        return np.ones(k)
    levels = np.array([10, -10, 5, -5, 0])
    if k % 512:
        return np.exp2(np.random.permutation(np.resize(levels, k // 32))).repeat(32)
    a = np.empty((k // 512, 16))
    for p in range(k // 512):
        a[p, :8] = np.random.permutation(np.resize(levels, 8))
        for g in range(8):
            far = levels[np.abs(levels - a[p, g]) >= 10]
            a[p, g + 8] = far[np.random.randint(len(far))]
    return np.exp2(a.ravel()).repeat(32)


def f64(x):
    return np.asarray(x).astype(np.float64)


def striped8(idx):
    return np.asarray(idx).reshape(8, -1, 16).transpose(0, 2, 1).reshape(128, -1).astype(np.uint16)


def unstriped8(offs):
    return offs.reshape(8, 16, -1).transpose(0, 2, 1).reshape(8, -1).astype(np.int64)


def pick8(x, idx, run):
    r = np.arange(len(x))
    return x[r[:, None], idx[r % (8 * run) // run]]


E2M1 = np.array([0.0, 0.5, 1.0, 1.5, 2.0, 3.0, 4.0, 6.0, -0.0, -0.5, -1.0, -1.5, -2.0, -3.0, -4.0, -6.0])


def pack_weight(w, fmt):
    k, n = w.shape
    w = f64(np.asarray(w, np.float32).astype(ml_dtypes.bfloat16)).reshape(k // 32, 32, n)
    amax = np.abs(w).max(1)
    if fmt == "e4m3":
        byte = np.frexp(amax)[1] - 1 + 127 - 7
    else:
        mant, ex = np.frexp(amax / 6.0)
        byte = np.where(mant > 0.5, ex, ex - 1) + 127
    byte = np.clip(np.where(amax > 0, byte, 1), 1, 254)
    scaled = (w * np.exp2(127.0 - byte)[:, None, :]).reshape(k, n).astype(np.float32)
    by_word = np.ascontiguousarray(scaled.reshape(k // 512, 128, 4, n).transpose(0, 1, 3, 2))
    if fmt == "e4m3":
        words = by_word.astype(ml_dtypes.float8_e4m3fn).view(np.uint8)
    else:
        c = by_word.astype(ml_dtypes.float4_e2m1fn).view(np.uint8) & 0xF
        words = (c[..., 0::2] | (c[..., 1::2] << 4)).reshape(k // 512, 128, 2 * n)
    return np.ascontiguousarray(words), np.ascontiguousarray(byte.astype(np.uint8).reshape(k // 512, 16, n))


def unpack_weight(words, scales, fmt):
    g, _, n = scales.shape
    words = np.ascontiguousarray(words).reshape(g, 128, n, -1)
    if fmt == "e4m3":
        vals = words.view(ml_dtypes.float8_e4m3fn).astype(np.float64)
    else:
        nib = np.empty((g, 128, n, 4), np.uint8)
        nib[..., 0::2] = words & 0xF
        nib[..., 1::2] = words >> 4
        vals = E2M1[nib]
    vals = vals * np.repeat(np.exp2(scales.astype(np.float64) - 127.0), 8, axis=1)[..., None]
    return vals.transpose(0, 1, 3, 2).reshape(g * 512, n)


D, E, T, Q, I, G = 512, 512, 1024, 128, 512, 64


def setup_inputs():
    n = np.random.standard_normal
    idx = np.stack([np.random.permutation(T)[:I] for _ in range(8)])
    fd = mx_kscale(D)
    fe = mx_kscale(E)
    keysp = pack_weight(n((D, T)) / fd[:, None], "e2m1")
    return {
        "query": (n((D, Q)) * 0.7 / np.sqrt(D) * fd[:, None]).astype(np.float32),
        "keys_words": keysp[0],
        "keys_scales": keysp[1],
        "gout": (n((E, Q)) * 1 / np.sqrt(E) * fe[:, None]).astype(np.float32),
        "vals": (n((E, T)) / fe[:, None]).astype(np.float32),
        "quota": (np.random.uniform(0.3, 2.0, (Q, G))).astype(np.float32),
        "dquery": (n((D, Q)) * 1.0 / np.sqrt(D) * fd[:, None]).astype(np.float32),
        "base": (0.5 * n((Q, T))).astype(np.float32),
        "offs": striped8(idx),
    }


def reference(query, keys_words, keys_scales, gout, vals, quota, dquery, base, offs):
    idx = unstriped8(offs)
    keysu = unpack_weight(keys_words, keys_scales, "e2m1")
    queryq = mxq(f64(query), 0, "e4m3")
    a = queryq.T @ keysu
    dqueryq = mxq(f64(dquery), 0, "e4m3")
    ta = dqueryq.T @ keysu
    p = np.exp(pick8(a, idx, 16))
    u1 = f64(quota) / p.reshape(Q, G, I // G).sum(axis=2)
    ur = np.repeat(u1, I // G, axis=1)
    goutq = mxq(f64(gout), 0, "e4m3")
    valsq = mxq(f64(vals), 0, "e4m3")
    c0 = goutq.T @ valsq
    dw = pick8(c0, idx, 16)
    dur = dw * p
    du1 = dur.reshape(Q, G, I // G).sum(axis=2)
    e1 = du1 * f64(quota) / np.square(p.reshape(Q, G, I // G).sum(axis=2)) * (-1.0)
    r1 = np.repeat(e1, I // G, axis=1)
    dp = dw * ur + r1
    xp = pick8(ta, idx, 16) * p
    xu1 = xp.reshape(Q, G, I // G).sum(axis=2) * f64(quota) / np.square(p.reshape(Q, G, I // G).sum(axis=2)) * (-1.0)
    xur = np.repeat(xu1, I // G, axis=1)
    xdur = xp * dw
    xdu1 = xdur.reshape(Q, G, I // G).sum(axis=2)
    xe1 = (xdu1 * f64(quota) - xp.reshape(Q, G, I // G).sum(axis=2) * p.reshape(Q, G, I // G).sum(axis=2) * 2.0 * du1 * f64(quota) / np.square(p.reshape(Q, G, I // G).sum(axis=2))) / np.square(p.reshape(Q, G, I // G).sum(axis=2)) * (-1.0)
    xr1 = np.repeat(xe1, I // G, axis=1)
    xdp = xur * dw + xr1
    xe2 = xdp * p + xp * dp
    xs2 = np.zeros((Q, T))
    xs2[np.arange(Q)[:, None], idx[np.arange(Q) % 128 // 16]] = xe2
    y = xs2 * 8.0 + f64(base)
    return y

@@ -1,0 +1,204 @@
+from contextlib import ExitStack
+
+import concourse.mybir as mybir
+
+F32 = mybir.dt.float32
+BF16 = mybir.dt.bfloat16
+I32 = mybir.dt.int32
+U32 = mybir.dt.uint32
+U16 = mybir.dt.uint16
+U8 = mybir.dt.uint8
+FP8X4 = mybir.dt.float8_e4m3fn_x4
+FP4X4 = mybir.dt.float4_e2m1fn_x4
+ALU = mybir.AluOpType
+ACT = mybir.ActivationFunctionType
+AX = mybir.AxisListType
+
+P = 128
+PACK = 4
+T = 1024
+Q = 128
+SLOTS = 512
+GROUPS = 64
+RUN = 8
+PARTS = 2
+PS = SLOTS // PARTS
+PG = GROUPS // PARTS
+VCH = 256
+FLOPS = 3 * 2 * 512 * Q * T
+
+
+def tile_attend_hvquota_heads_kernel(tc, query, keys_words, keys_scales, gout, vals, quota, dquery, base, offs, out):
+    nc = tc.nc
+    with ExitStack() as ctx:
+        keep = ctx.enter_context(tc.tile_pool(name="keep", bufs=1))
+        psum = ctx.enter_context(tc.psum_pool(name="psum", bufs=1))
+
+        def sb(name, shape, dtype=F32):
+            return keep.tile(shape, dtype, name=name, align_bytes=64)
+
+        offsets = keep.tile([P, SLOTS // 16], U16, name="offsets")
+        key_scales = sb("key_scales", [P, T], U8)
+        scattered = sb("scattered", [P, T])
+        nc.gpsimd.memset(key_scales[:].bitcast(I32), 0)
+        nc.vector.memset(scattered[:], 0.0)
+
+        warm = sb("warm", [P, 8])
+        nc.scalar.activation(out=warm[:, 0:1], in_=scattered[:, 0:1], func=ACT.Exp)
+
+        def load_rows(name, rows):
+            raw = sb(name, [P, PACK, rows.shape[1]])
+            nc.sync.dma_start(out=raw[:], in_=rows.rearrange("(p j) w -> p j w", j=PACK))
+            return raw
+
+        def interleave(name, raw, on_scalar):
+            width = raw.shape[2]
+            woven = sb(name, [P, width, PACK], BF16)
+            dst = woven[:].rearrange("p (c i) j -> p c j i", i=4)
+            src = raw[:].rearrange("p j (c i) -> p c j i", i=4)
+            if on_scalar:
+                nc.scalar.copy(out=dst, in_=src)
+            else:
+                nc.vector.tensor_copy(out=dst, in_=src)
+            return woven
+
+        def quantize(name, woven):
+            width = woven.shape[1]
+            codes = sb(name + "_codes", [P, width], U32)
+            scales = sb(name + "_scales", [P, width], U8)
+            nc.vector.quantize_mx(out=codes[:].bitcast(FP8X4), scales=scales[:], in_=woven[:].rearrange("p w j -> p (w j)"))
+            return codes, scales
+
+        def load_scales():
+            for quad in range(4):
+                nc.sync.dma_start(out=key_scales[32 * quad : 32 * quad + 4, :].bitcast(I32), in_=keys_scales[0, 4 * quad : 4 * quad + 4, :].bitcast(I32))
+
+        load_scales()
+        q_raw = load_rows("q_raw", query)
+        key_words = sb("key_words", [P, 2 * T], U8)
+
+        nc.sync.dma_start(out=key_words[:].bitcast(I32), in_=keys_words[0].bitcast(I32))
+        dq_raw = load_rows("dq_raw", dquery)
+        nc.sync.dma_start(offsets[:], offs)
+        g_raw = load_rows("g_raw", gout)
+        quota_sb = sb("quota_sb", [P, GROUPS])
+        nc.sync.dma_start(out=quota_sb[:], in_=quota)
+        v_raw = [load_rows("v_raw%d" % c, vals[:, c * VCH : (c + 1) * VCH]) for c in range(T // VCH)]
+        base_sb = sb("base_sb", [P, T])
+        nc.sync.dma_start(out=base_sb[:], in_=base)
+
+        def scores(name, q, engines, tag0):
+            whole = sb(name, [P, T])
+            n = T // len(engines)
+            for h in range(len(engines)):
+                acc = psum.tile([P, 512], F32, name="%s_ps%d" % (name, h), tag="bank%d" % (tag0 + h))
+                nc.tensor.matmul_mx(out=acc[:, :n], lhsT=q[0][:].bitcast(FP8X4), lhsT_scale=q[1][:],
+                                    rhs=key_words[:, 2 * n * h : 2 * n * (h + 1)].bitcast(FP4X4),
+                                    rhs_scale=key_scales[:, n * h : n * (h + 1)], start=True, stop=True)
+                if engines[h] == "s":
+                    nc.scalar.copy(out=whole[:, n * h : n * (h + 1)], in_=acc[:, :n])
+                else:
+                    nc.vector.tensor_copy(out=whole[:, n * h : n * (h + 1)], in_=acc[:, :n])
+            return whole
+
+        parts = range(PARTS)
+
+        def slot_tiles(name):
+            return [sb("%s%d" % (name, h), [P, PS]) for h in parts]
+
+        def group_tiles(name):
+            return [sb("%s%d" % (name, h), [P, PG]) for h in parts]
+
+        def grouped(t):
+            return t[:].rearrange("p (g r) -> p g r", r=RUN)
+
+        def spread(t):
+            return t.unsqueeze(2).to_broadcast([P, PG, RUN])
+
+        def listed(window, h):
+            return window[:].indirect(offsets[:, h * PS // 16 : (h + 1) * PS // 16])
+
+        def group_reduce(name, src, op, negate=None):
+            dst = group_tiles(name)
+            for h in parts:
+                nc.vector.tensor_reduce(out=dst[h][:], in_=grouped(src[h]), axis=AX.X, op=op, negate=negate)
+            return dst
+
+        def with_group(name, src, per_group, op):
+            dst = slot_tiles(name)
+            for h in parts:
+                nc.vector.tensor_tensor(grouped(dst[h]), grouped(src[h]), spread(per_group[h][:]), op)
+            return dst
+
+        def pair(name, x, y, op):
+            dst = slot_tiles(name)
+            for h in parts:
+                nc.vector.tensor_tensor(dst[h][:], x[h][:], y[h][:], op)
+            return dst
+
+        def gathered_times(name, window, y):
+            dst = slot_tiles(name)
+            for h in parts:
+                nc.vector.tensor_tensor(dst[h][:], listed(window, h), y[h][:], ALU.mult)
+            return dst
+
+        qq = quantize("q", interleave("q_il", q_raw, False))
+        dqq = quantize("dq", interleave("dq_il", dq_raw, False))
+        a = scores("a", qq, "svsv", 0)
+        gq = quantize("g", interleave("g_il", g_raw, False))
+        ta = scores("ta", dqq, "ss", 4)
+
+        quota_slots = slot_tiles("quota_slots")
+        for h in parts:
+            nc.scalar.copy(out=grouped(quota_slots[h]), in_=spread(quota_sb[:, h * PG : (h + 1) * PG]))
+
+        ag = slot_tiles("ag")
+        for h in parts:
+            nc.vector.tensor_copy(ag[h][:], listed(a, h))
+        neg_max = group_reduce("neg_max", ag, ALU.max, True)
+        shifted = with_group("shifted", ag, neg_max, ALU.add)
+        p = slot_tiles("p")
+        for h in parts:
+            nc.scalar.activation(out=p[h][:], in_=shifted[h][:], func=ACT.Exp)
+
+        c0 = sb("c0", [P, T])
+        woven = [interleave("v_il%d" % c, v_raw[c], "ssss"[c] == "s") for c in range(T // VCH)]
+
+        def values(c):
+            vq = quantize("v%d" % c, woven[c])
+            acc = psum.tile([P, 512], F32, name="c_ps%d" % c, tag="bank%d" % ((6 + c) % 8))
+            nc.tensor.matmul_mx(out=acc[:, :VCH], lhsT=gq[0][:].bitcast(FP8X4), lhsT_scale=gq[1][:],
+                                rhs=vq[0][:].bitcast(FP8X4), rhs_scale=vq[1][:], start=True, stop=True)
+            nc.scalar.copy(out=c0[:, c * VCH : (c + 1) * VCH], in_=acc[:, :VCH])
+
+        total = group_reduce("total", p, ALU.add)
+        inv = group_tiles("inv")
+        for h in parts:
+            nc.vector.reciprocal(inv[h][:], total[h][:])
+        for c in range(2):
+            values(c)
+        w = with_group("w", p, inv, ALU.mult)
+        wt = gathered_times("wt", ta, w)
+        t_mean = group_reduce("t_mean", wt, ALU.add)
+        for c in range(2, T // VCH):
+            values(c)
+        w_mean = with_group("w_mean", w, t_mean, ALU.mult)
+        u = pair("u", wt, w_mean, ALU.subtract)
+
+        d = gathered_times("d", c0, quota_slots)
+        wd = pair("wd", w, d, ALU.mult)
+        d_mean = group_reduce("d_mean", wd, ALU.add)
+        dc = with_group("dc", d, d_mean, ALU.subtract)
+        ue = pair("ue", u, dc, ALU.mult)
+        neg_cov = group_reduce("neg_cov", ue, ALU.add, True)
+        wc = with_group("wc", w, neg_cov, ALU.mult)
+        for h in parts:
+            nc.vector.tensor_tensor(listed(scattered, h), ue[h][:], wc[h][:], ALU.add)
+
+        c_lo = 0
+        for c, n in enumerate([512,512]):
+            cols = slice(c_lo, c_lo + n)
+            c_lo = c_lo + n
+            res = sb("res%d" % c, [P, n])
+            nc.vector.scalar_tensor_tensor(out=res[:], in0=scattered[:, cols], scalar=8.0, in1=base_sb[:, cols], op0=ALU.mult, op1=ALU.add)
+            (nc.sync if c % 2 == 0 else nc.scalar).dma_start(out=out[:, cols], in_=res[:])

@@ -25,6 +25,7 @@ PARTS = 2
 PS = SLOTS // PARTS
 PG = GROUPS // PARTS
 VCH = 256
+TIES = {"c0":"v_raw3","w_mean":"v_il3"}
 FLOPS = 3 * 2 * 512 * Q * T
 
 
@@ -35,16 +36,18 @@ def tile_attend_hvquota_heads_kernel(tc, query, keys_words, keys_scales, gout, v
         psum = ctx.enter_context(tc.psum_pool(name="psum", bufs=1))
 
         def sb(name, shape, dtype=F32):
-            return keep.tile(shape, dtype, name=name, align_bytes=64)
+            return keep.tile(shape, dtype, name=name, tag=TIES.get(name, name), align_bytes=64)
 
         offsets = keep.tile([P, SLOTS // 16], U16, name="offsets")
         key_scales = sb("key_scales", [P, T], U8)
         scattered = sb("scattered", [P, T])
         nc.gpsimd.memset(key_scales[:].bitcast(I32), 0)
-        nc.vector.memset(scattered[:], 0.0)
 
         warm = sb("warm", [P, 8])
-        nc.scalar.activation(out=warm[:, 0:1], in_=scattered[:, 0:1], func=ACT.Exp)
+        nc.vector.memset(warm[:, 4:5], 0.0)
+        nc.scalar.activation(out=warm[:, 0:1], in_=warm[:, 4:5], func=ACT.Exp)
+
+        nc.vector.memset(scattered[:], 0.0)
 
         def load_rows(name, rows):
             raw = sb(name, [P, PACK, rows.shape[1]])
@@ -54,12 +57,16 @@ def tile_attend_hvquota_heads_kernel(tc, query, keys_words, keys_scales, gout, v
         def interleave(name, raw, on_scalar):
             width = raw.shape[2]
             woven = sb(name, [P, width, PACK], BF16)
-            dst = woven[:].rearrange("p (c i) j -> p c j i", i=4)
-            src = raw[:].rearrange("p j (c i) -> p c j i", i=4)
-            if on_scalar:
-                nc.scalar.copy(out=dst, in_=src)
-            else:
-                nc.vector.tensor_copy(out=dst, in_=src)
+            n = width // len(on_scalar)
+            for k, eng in enumerate(on_scalar):
+                dst = woven[:, k * n : (k + 1) * n, :].rearrange("p (c i) j -> p c j i", i=4)
+                src = raw[:, :, k * n : (k + 1) * n].rearrange("p j (c i) -> p c j i", i=4)
+                if eng == "g":
+                    nc.gpsimd.tensor_scalar(dst, src, 1.0, 0.0, ALU.mult, ALU.add)
+                elif eng == "s":
+                    nc.scalar.copy(out=dst, in_=src)
+                else:
+                    nc.vector.tensor_copy(out=dst, in_=src)
             return woven
 
         def quantize(name, woven):
@@ -79,11 +86,14 @@ def tile_attend_hvquota_heads_kernel(tc, query, keys_words, keys_scales, gout, v
 
         nc.sync.dma_start(out=key_words[:].bitcast(I32), in_=keys_words[0].bitcast(I32))
         dq_raw = load_rows("dq_raw", dquery)
-        nc.sync.dma_start(offsets[:], offs)
         g_raw = load_rows("g_raw", gout)
         quota_sb = sb("quota_sb", [P, GROUPS])
-        nc.sync.dma_start(out=quota_sb[:], in_=quota)
-        v_raw = [load_rows("v_raw%d" % c, vals[:, c * VCH : (c + 1) * VCH]) for c in range(T // VCH)]
+        nc.sync.dma_start(offsets[:], offs)
+        v_raw = []
+        for c in range(T // VCH):
+            v_raw.append(load_rows("v_raw%d" % c, vals[:, c * VCH : (c + 1) * VCH]))
+            if c == 0:
+                nc.sync.dma_start(out=quota_sb[:], in_=quota)
         base_sb = sb("base_sb", [P, T])
         nc.sync.dma_start(out=base_sb[:], in_=base)
 
@@ -104,6 +114,9 @@ def tile_attend_hvquota_heads_kernel(tc, query, keys_words, keys_scales, gout, v
         parts = range(PARTS)
 
         def slot_tiles(name):
+            if name == "w_mean":
+                joined = sb(name, [P, SLOTS])
+                return [joined[:, h * PS : (h + 1) * PS] for h in parts]
             return [sb("%s%d" % (name, h), [P, PS]) for h in parts]
 
         def group_tiles(name):
@@ -142,10 +155,10 @@ def tile_attend_hvquota_heads_kernel(tc, query, keys_words, keys_scales, gout, v
                 nc.vector.tensor_tensor(dst[h][:], listed(window, h), y[h][:], ALU.mult)
             return dst
 
-        qq = quantize("q", interleave("q_il", q_raw, False))
-        dqq = quantize("dq", interleave("dq_il", dq_raw, False))
+        qq = quantize("q", interleave("q_il", q_raw, "v"))
+        dqq = quantize("dq", interleave("dq_il", dq_raw, "v"))
         a = scores("a", qq, "svsv", 0)
-        gq = quantize("g", interleave("g_il", g_raw, False))
+        g_il = interleave("g_il", g_raw, "g")
         ta = scores("ta", dqq, "ss", 4)
 
         quota_slots = slot_tiles("quota_slots")
@@ -161,8 +174,9 @@ def tile_attend_hvquota_heads_kernel(tc, query, keys_words, keys_scales, gout, v
         for h in parts:
             nc.scalar.activation(out=p[h][:], in_=shifted[h][:], func=ACT.Exp)
 
+        gq = quantize("g", g_il)
         c0 = sb("c0", [P, T])
-        woven = [interleave("v_il%d" % c, v_raw[c], "ssss"[c] == "s") for c in range(T // VCH)]
+        woven = [interleave("v_il%d" % c, v_raw[c], "gg,ss,s,s".split(",")[c]) for c in range(T // VCH)]
 
         def values(c):
             vq = quantize("v%d" % c, woven[c])
@@ -196,7 +210,7 @@ def tile_attend_hvquota_heads_kernel(tc, query, keys_words, keys_scales, gout, v
             nc.vector.tensor_tensor(listed(scattered, h), ue[h][:], wc[h][:], ALU.add)
 
         c_lo = 0
-        for c, n in enumerate([512,512]):
+        for c, n in enumerate([512,256,256]):
             cols = slice(c_lo, c_lo + n)
             c_lo = c_lo + n
             res = sb("res%d" % c, [P, n])

from contextlib import ExitStack

import concourse.mybir as mybir

F32 = mybir.dt.float32
BF16 = mybir.dt.bfloat16
I32 = mybir.dt.int32
U32 = mybir.dt.uint32
U16 = mybir.dt.uint16
U8 = mybir.dt.uint8
FP8X4 = mybir.dt.float8_e4m3fn_x4
FP4X4 = mybir.dt.float4_e2m1fn_x4
ALU = mybir.AluOpType
ACT = mybir.ActivationFunctionType
AX = mybir.AxisListType

P = 128
PACK = 4
T = 1024
Q = 128
SLOTS = 512
GROUPS = 64
RUN = 8
PARTS = 2
PS = SLOTS // PARTS
PG = GROUPS // PARTS
VCH = 256
TIES = {"c0":"v_raw3","w_mean":"v_il3"}
FLOPS = 3 * 2 * 512 * Q * T


def tile_attend_hvquota_heads_kernel(tc, query, keys_words, keys_scales, gout, vals, quota, dquery, base, offs, out):
    nc = tc.nc
    with ExitStack() as ctx:
        keep = ctx.enter_context(tc.tile_pool(name="keep", bufs=1))
        psum = ctx.enter_context(tc.psum_pool(name="psum", bufs=1))

        def sb(name, shape, dtype=F32):
            return keep.tile(shape, dtype, name=name, tag=TIES.get(name, name), align_bytes=64)

        offsets = keep.tile([P, SLOTS // 16], U16, name="offsets")
        key_scales = sb("key_scales", [P, T], U8)
        scattered = sb("scattered", [P, T])
        nc.gpsimd.memset(key_scales[:].bitcast(I32), 0)

        warm = sb("warm", [P, 8])
        nc.vector.memset(warm[:, 4:5], 0.0)
        nc.scalar.activation(out=warm[:, 0:1], in_=warm[:, 4:5], func=ACT.Exp)

        nc.vector.memset(scattered[:], 0.0)

        def load_rows(name, rows):
            raw = sb(name, [P, PACK, rows.shape[1]])
            nc.sync.dma_start(out=raw[:], in_=rows.rearrange("(p j) w -> p j w", j=PACK))
            return raw

        def interleave(name, raw, on_scalar):
            width = raw.shape[2]
            woven = sb(name, [P, width, PACK], BF16)
            n = width // len(on_scalar)
            for k, eng in enumerate(on_scalar):
                dst = woven[:, k * n : (k + 1) * n, :].rearrange("p (c i) j -> p c j i", i=4)
                src = raw[:, :, k * n : (k + 1) * n].rearrange("p j (c i) -> p c j i", i=4)
                if eng == "g":
                    nc.gpsimd.tensor_scalar(dst, src, 1.0, 0.0, ALU.mult, ALU.add)
                elif eng == "s":
                    nc.scalar.copy(out=dst, in_=src)
                else:
                    nc.vector.tensor_copy(out=dst, in_=src)
            return woven

        def quantize(name, woven):
            width = woven.shape[1]
            codes = sb(name + "_codes", [P, width], U32)
            scales = sb(name + "_scales", [P, width], U8)
            nc.vector.quantize_mx(out=codes[:].bitcast(FP8X4), scales=scales[:], in_=woven[:].rearrange("p w j -> p (w j)"))
            return codes, scales

        def load_scales():
            for quad in range(4):
                nc.sync.dma_start(out=key_scales[32 * quad : 32 * quad + 4, :].bitcast(I32), in_=keys_scales[0, 4 * quad : 4 * quad + 4, :].bitcast(I32))

        load_scales()
        q_raw = load_rows("q_raw", query)
        key_words = sb("key_words", [P, 2 * T], U8)

        nc.sync.dma_start(out=key_words[:].bitcast(I32), in_=keys_words[0].bitcast(I32))
        dq_raw = load_rows("dq_raw", dquery)
        g_raw = load_rows("g_raw", gout)
        quota_sb = sb("quota_sb", [P, GROUPS])
        nc.sync.dma_start(offsets[:], offs)
        v_raw = []
        for c in range(T // VCH):
            v_raw.append(load_rows("v_raw%d" % c, vals[:, c * VCH : (c + 1) * VCH]))
            if c == 0:
                nc.sync.dma_start(out=quota_sb[:], in_=quota)
        base_sb = sb("base_sb", [P, T])
        nc.sync.dma_start(out=base_sb[:], in_=base)

        def scores(name, q, engines, tag0):
            whole = sb(name, [P, T])
            n = T // len(engines)
            for h in range(len(engines)):
                acc = psum.tile([P, 512], F32, name="%s_ps%d" % (name, h), tag="bank%d" % (tag0 + h))
                nc.tensor.matmul_mx(out=acc[:, :n], lhsT=q[0][:].bitcast(FP8X4), lhsT_scale=q[1][:],
                                    rhs=key_words[:, 2 * n * h : 2 * n * (h + 1)].bitcast(FP4X4),
                                    rhs_scale=key_scales[:, n * h : n * (h + 1)], start=True, stop=True)
                if engines[h] == "s":
                    nc.scalar.copy(out=whole[:, n * h : n * (h + 1)], in_=acc[:, :n])
                else:
                    nc.vector.tensor_copy(out=whole[:, n * h : n * (h + 1)], in_=acc[:, :n])
            return whole

        parts = range(PARTS)

        def slot_tiles(name):
            if name == "w_mean":
                joined = sb(name, [P, SLOTS])
                return [joined[:, h * PS : (h + 1) * PS] for h in parts]
            return [sb("%s%d" % (name, h), [P, PS]) for h in parts]

        def group_tiles(name):
            return [sb("%s%d" % (name, h), [P, PG]) for h in parts]

        def grouped(t):
            return t[:].rearrange("p (g r) -> p g r", r=RUN)

        def spread(t):
            return t.unsqueeze(2).to_broadcast([P, PG, RUN])

        def listed(window, h):
            return window[:].indirect(offsets[:, h * PS // 16 : (h + 1) * PS // 16])

        def group_reduce(name, src, op, negate=None):
            dst = group_tiles(name)
            for h in parts:
                nc.vector.tensor_reduce(out=dst[h][:], in_=grouped(src[h]), axis=AX.X, op=op, negate=negate)
            return dst

        def with_group(name, src, per_group, op):
            dst = slot_tiles(name)
            for h in parts:
                nc.vector.tensor_tensor(grouped(dst[h]), grouped(src[h]), spread(per_group[h][:]), op)
            return dst

        def pair(name, x, y, op):
            dst = slot_tiles(name)
            for h in parts:
                nc.vector.tensor_tensor(dst[h][:], x[h][:], y[h][:], op)
            return dst

        def gathered_times(name, window, y):
            dst = slot_tiles(name)
            for h in parts:
                nc.vector.tensor_tensor(dst[h][:], listed(window, h), y[h][:], ALU.mult)
            return dst

        qq = quantize("q", interleave("q_il", q_raw, "v"))
        dqq = quantize("dq", interleave("dq_il", dq_raw, "v"))
        a = scores("a", qq, "svsv", 0)
        g_il = interleave("g_il", g_raw, "g")
        ta = scores("ta", dqq, "ss", 4)

        quota_slots = slot_tiles("quota_slots")
        for h in parts:
            nc.scalar.copy(out=grouped(quota_slots[h]), in_=spread(quota_sb[:, h * PG : (h + 1) * PG]))

        ag = slot_tiles("ag")
        for h in parts:
            nc.vector.tensor_copy(ag[h][:], listed(a, h))
        neg_max = group_reduce("neg_max", ag, ALU.max, True)
        shifted = with_group("shifted", ag, neg_max, ALU.add)
        p = slot_tiles("p")
        for h in parts:
            nc.scalar.activation(out=p[h][:], in_=shifted[h][:], func=ACT.Exp)

        gq = quantize("g", g_il)
        c0 = sb("c0", [P, T])
        woven = [interleave("v_il%d" % c, v_raw[c], "gg,ss,s,s".split(",")[c]) for c in range(T // VCH)]

        def values(c):
            vq = quantize("v%d" % c, woven[c])
            acc = psum.tile([P, 512], F32, name="c_ps%d" % c, tag="bank%d" % ((6 + c) % 8))
            nc.tensor.matmul_mx(out=acc[:, :VCH], lhsT=gq[0][:].bitcast(FP8X4), lhsT_scale=gq[1][:],
                                rhs=vq[0][:].bitcast(FP8X4), rhs_scale=vq[1][:], start=True, stop=True)
            nc.scalar.copy(out=c0[:, c * VCH : (c + 1) * VCH], in_=acc[:, :VCH])

        total = group_reduce("total", p, ALU.add)
        inv = group_tiles("inv")
        for h in parts:
            nc.vector.reciprocal(inv[h][:], total[h][:])
        for c in range(2):
            values(c)
        w = with_group("w", p, inv, ALU.mult)
        wt = gathered_times("wt", ta, w)
        t_mean = group_reduce("t_mean", wt, ALU.add)
        for c in range(2, T // VCH):
            values(c)
        w_mean = with_group("w_mean", w, t_mean, ALU.mult)
        u = pair("u", wt, w_mean, ALU.subtract)

        d = gathered_times("d", c0, quota_slots)
        wd = pair("wd", w, d, ALU.mult)
        d_mean = group_reduce("d_mean", wd, ALU.add)
        dc = with_group("dc", d, d_mean, ALU.subtract)
        ue = pair("ue", u, dc, ALU.mult)
        neg_cov = group_reduce("neg_cov", ue, ALU.add, True)
        wc = with_group("wc", w, neg_cov, ALU.mult)
        for h in parts:
            nc.vector.tensor_tensor(listed(scattered, h), ue[h][:], wc[h][:], ALU.add)

        c_lo = 0
        for c, n in enumerate([512,256,256]):
            cols = slice(c_lo, c_lo + n)
            c_lo = c_lo + n
            res = sb("res%d" % c, [P, n])
            nc.vector.scalar_tensor_tensor(out=res[:], in0=scattered[:, cols], scalar=8.0, in1=base_sb[:, cols], op0=ALU.mult, op1=ALU.add)
            (nc.sync if c % 2 == 0 else nc.scalar).dma_start(out=out[:, cols], in_=res[:])
